import numpy as np
import ml_dtypes


def mxq(x, axis, fmt="e4m3"):
    dtype, down = {"e4m3": (ml_dtypes.float8_e4m3fn, 7), "e5m2": (ml_dtypes.float8_e5m2, 14)}[fmt]
    v = np.moveaxis(np.asarray(x, np.float32).astype(ml_dtypes.bfloat16).astype(np.float64), axis, -1)
    blocks = v.reshape(v.shape[:-1] + (-1, 32))
    amax = np.abs(blocks).max(-1, keepdims=True)
    byte = np.maximum(np.where(amax > 0, np.frexp(amax)[1] - 1 + 127, 0) - down, 1)
    scale = np.exp2(byte - 127.0)
    codes = (blocks / scale).astype(np.float32).astype(dtype).astype(np.float64)
    return np.moveaxis((codes * scale).reshape(v.shape), -1, axis)


WIDE = False


def mx_kscale(k):
    if not WIDE:
        return np.ones(k)
    levels = np.array([10, -10, 5, -5, 0])
    if k % 512:
        return np.exp2(np.random.permutation(np.resize(levels, k // 32))).repeat(32)
    a = np.empty((k // 512, 16))
    for p in range(k // 512):
        a[p, :8] = np.random.permutation(np.resize(levels, 8))
        for g in range(8):
            far = levels[np.abs(levels - a[p, g]) >= 10]
            a[p, g + 8] = far[np.random.randint(len(far))]
    return np.exp2(a.ravel()).repeat(32)


def f64(x):
    return np.asarray(x).astype(np.float64)


E2M1 = np.array([0.0, 0.5, 1.0, 1.5, 2.0, 3.0, 4.0, 6.0, -0.0, -0.5, -1.0, -1.5, -2.0, -3.0, -4.0, -6.0])


def pack_weight(w, fmt):
    k, n = w.shape
    w = f64(np.asarray(w, np.float32).astype(ml_dtypes.bfloat16)).reshape(k // 32, 32, n)
    amax = np.abs(w).max(1)
    if fmt == "e4m3":
        byte = np.frexp(amax)[1] - 1 + 127 - 7
    else:
        mant, ex = np.frexp(amax / 6.0)
        byte = np.where(mant > 0.5, ex, ex - 1) + 127
    byte = np.clip(np.where(amax > 0, byte, 1), 1, 254)
    scaled = (w * np.exp2(127.0 - byte)[:, None, :]).reshape(k, n).astype(np.float32)
    by_word = np.ascontiguousarray(scaled.reshape(k // 512, 128, 4, n).transpose(0, 1, 3, 2))
    if fmt == "e4m3":
        words = by_word.astype(ml_dtypes.float8_e4m3fn).view(np.uint8)
    else:
        c = by_word.astype(ml_dtypes.float4_e2m1fn).view(np.uint8) & 0xF
        words = (c[..., 0::2] | (c[..., 1::2] << 4)).reshape(k // 512, 128, 2 * n)
    return np.ascontiguousarray(words), np.ascontiguousarray(byte.astype(np.uint8).reshape(k // 512, 16, n))


def unpack_weight(words, scales, fmt):
    g, _, n = scales.shape
    words = np.ascontiguousarray(words).reshape(g, 128, n, -1)
    if fmt == "e4m3":
        vals = words.view(ml_dtypes.float8_e4m3fn).astype(np.float64)
    else:
        nib = np.empty((g, 128, n, 4), np.uint8)
        nib[..., 0::2] = words & 0xF
        nib[..., 1::2] = words >> 4
        vals = E2M1[nib]
    vals = vals * np.repeat(np.exp2(scales.astype(np.float64) - 127.0), 8, axis=1)[..., None]
    return vals.transpose(0, 1, 3, 2).reshape(g * 512, n)


def bf(x):
    return np.asarray(x, np.float32).astype(ml_dtypes.bfloat16)


def planes(Y):
    r, m = Y.shape
    b = f64(bf(Y)).reshape(r // 32, 32, m)
    amax = np.abs(b).max(1)
    byte = np.clip(np.where(amax > 0, np.frexp(amax)[1] - 1 + 127 - 7, 1), 1, 254)
    codes = (b * np.exp2(127.0 - byte)[:, None, :]).reshape(r, m).astype(np.float32).astype(ml_dtypes.float8_e4m3fn).view(np.uint8)
    words = codes.reshape(r // 512, 128, 4, m).transpose(0, 1, 3, 2)
    return np.ascontiguousarray(words), np.ascontiguousarray(byte.astype(np.uint8).reshape(r // 512, 16, m))


K, L, T, R, N = 1024, 512, 512, 512, 512


def setup_inputs():
    n = np.random.standard_normal
    fk = mx_kscale(K)
    fl = mx_kscale(L)
    fr = mx_kscale(R)
    xtp = pack_weight(n((K, T)) / fk[:, None], "e2m1")
    wap = pack_weight(n((K, R)) * 1 / np.sqrt(K) * fk[:, None], "e4m3")
    xqp = pack_weight(n((L, T)) / fl[:, None], "e2m1")
    wcp = pack_weight(n((L, R)) * 1 / np.sqrt(L) * fl[:, None], "e4m3")
    wbp = pack_weight(n((R, N)) * 1 / np.sqrt(R) / fr[:, None], "e2m1")
    wyp = pack_weight(n((K, N)) * 1 / np.sqrt(K) * fk[:, None], "e4m3")
    return {
        "xt_words": xtp[0],
        "xt_scales": xtp[1],
        "wa_words": wap[0],
        "wa_scales": wap[1],
        "xq_words": xqp[0],
        "xq_scales": xqp[1],
        "wc_words": wcp[0],
        "wc_scales": wcp[1],
        "us": (np.random.uniform(0.5, 2.0, (R, 1)) * fr[:, None]).astype(np.float32),
        "wb_words": wbp[0],
        "wb_scales": wbp[1],
        "wy_words": wyp[0],
        "wy_scales": wyp[1],
    }


def reference(xt_words, xt_scales, wa_words, wa_scales, xq_words, xq_scales, wc_words, wc_scales, us, wb_words, wb_scales, wy_words, wy_scales):
    xtu = unpack_weight(xt_words, xt_scales, "e2m1")
    wau = unpack_weight(wa_words, wa_scales, "e4m3")
    xqu = unpack_weight(xq_words, xq_scales, "e2m1")
    wcu = unpack_weight(wc_words, wc_scales, "e4m3")
    wbu = unpack_weight(wb_words, wb_scales, "e2m1")
    wyu = unpack_weight(wy_words, wy_scales, "e4m3")
    a = wau.T @ xtu
    b = wcu.T @ xqu
    hid = a / (1.0 + np.abs(b)) * f64(us)
    hidq = mxq(hid, 0, "e4m3")
    y = wbu.T @ hidq + wyu.T @ xtu
    words, scales = planes(y)
    return y, words, scales

@@ -1,0 +1,295 @@
+from contextlib import ExitStack
+
+import concourse.mybir as mybir
+
+F32 = mybir.dt.float32
+BF16 = mybir.dt.bfloat16
+I32 = mybir.dt.int32
+U8 = mybir.dt.uint8
+FP8X4 = mybir.dt.float8_e4m3fn_x4
+FP4X4 = mybir.dt.float4_e2m1fn_x4
+ACT = mybir.ActivationFunctionType
+ALU = mybir.AluOpType
+
+K, L, T, R, N = 1024, 512, 512, 512, 512
+P = 128
+PACK = 4
+W = 512
+TC = 128
+CHUNKS = T // TC
+FLOPS = 2 * T * (K * R + L * R + R * N + K * N)
+
+
+def tile_mix_hidden_divided_hidden_pl_kernel(
+    tc, xt_words, xt_scales, wa_words, wa_scales, xq_words, xq_scales, wc_words, wc_scales,
+    us, wb_words, wb_scales, wy_words, wy_scales, out_0, out_1, out_2,
+):
+    nc = tc.nc
+    with ExitStack() as ctx:
+        keep = ctx.enter_context(tc.tile_pool(name="keep", bufs=1))
+        psum = ctx.enter_context(tc.psum_pool(name="psum", bufs=1))
+        ctx.enter_context(tc.manual_schedule())
+
+        def sb(name, shape, dtype):
+            return keep.tile(shape, dtype, name=name, align_bytes=64)
+
+        def plane(name, passes):
+            t = sb(name, [P, passes * W], U8)
+            nc.vector.memset(t[:].bitcast(I32), 0)
+            return t
+
+        def load_scales(queue, t, scales, quads=range(4)):
+            passes = scales.shape[0]
+            for q in quads:
+                queue.dma_start(
+                    out=t[32 * q : 32 * q + 4, :].bitcast(I32).rearrange("r (g c) -> r g c", g=passes),
+                    in_=scales[:, 4 * q : 4 * q + 4, :].bitcast(I32).rearrange("g r c -> r g c"),
+                )
+
+        def load_fp8(queue, name, words):
+            passes = words.shape[0]
+            t = sb(name, [P, passes * W], I32)
+            queue.dma_start(
+                out=t[:].rearrange("p (g c) -> p g c", g=passes),
+                in_=words.rearrange("g p c t -> p g (c t)").bitcast(I32),
+            )
+            return t
+
+        def load_fp4(queue, name, words):
+            passes = words.shape[0]
+            t = sb(name, [P, passes * 2 * W], U8)
+            queue.dma_start(
+                out=t[:].bitcast(I32).rearrange("p (g c) -> p g c", g=passes),
+                in_=words.bitcast(I32).rearrange("g p c -> p g c"),
+            )
+            return t
+
+        def deal_words(name, raw, g):
+            t = sb(name, [P, W], I32)
+            nc.vector.tensor_copy(
+                out=t[:].rearrange("p (j b k) -> p b j k", j=PACK, k=4),
+                in_=raw[:, g * W : (g + 1) * W].rearrange("p (b k j) -> p b j k", j=PACK, k=4),
+            )
+            return t
+
+        def deal_scales(name, raw, passes):
+            t = sb(name, [P, passes * W], U8)
+            nc.vector.tensor_copy(
+                out=t[:].rearrange("p (g j b k) -> p g b j k", g=passes, j=PACK, k=16),
+                in_=raw[:].rearrange("p (g b k j) -> p g b j k", g=passes, j=PACK, k=16),
+            )
+            return t
+
+        def deal_fp4(name, raw):
+            t = sb(name, [P, 2 * W], U8)
+            nc.vector.tensor_copy(
+                out=t[:].rearrange("p (j b k e) -> p b j k e", j=PACK, k=8, e=2),
+                in_=raw[:].rearrange("p (b k j e) -> p b j k e", j=PACK, k=8, e=2),
+            )
+            return t
+
+        def fp8(t, c0):
+            return t[:, c0 : c0 + P].bitcast(FP8X4)
+
+        def fp4(t, c0):
+            return t[:, 2 * c0 : 2 * (c0 + P)].bitcast(FP4X4)
+
+        def cols(t, c0):
+            return t[:, c0 : c0 + P]
+
+        wc_s_raw = plane("wc_s_raw", 1)
+        xq_s = plane("xq_s", 1)
+        wa_s_raw = plane("wa_s_raw", 2)
+        xt_s = plane("xt_s", 2)
+        wb_s_raw = plane("wb_s_raw", 1)
+        wy_s_raw = plane("wy_s_raw", 2)
+
+        one = sb("one", [P, 1], F32)
+        nc.gpsimd.memset(one[:], 1.0)
+        us_t = sb("us_t", [P, PACK], F32)
+        nc.gpsimd.dma_start(out=us_t[:], in_=us.rearrange("(p j) o -> p (j o)", j=PACK))
+
+        wc_raw = load_fp8(nc.scalar, "wc_raw", wc_words)
+        xq = load_fp4(nc.scalar, "xq", xq_words)
+        load_scales(nc.sync, wc_s_raw, wc_scales)
+        load_scales(nc.sync, xq_s, xq_scales)
+        wa_raw = load_fp8(nc.sync, "wa_raw", wa_words)
+        load_scales(nc.sync, wa_s_raw, wa_scales)
+        xt = load_fp4(nc.sync, "xt", xt_words)
+        load_scales(nc.sync, xt_s, xt_scales)
+        wb_raw = load_fp4(nc.sync, "wb_raw", wb_words)
+        wy_raw = load_fp8(nc.sync, "wy_raw", wy_words)
+        load_scales(nc.sync, wb_s_raw, wb_scales)
+        load_scales(nc.sync, wy_s_raw, wy_scales)
+
+        warm = sb("warm", [P, 1], F32)
+        nc.scalar.activation(out=warm[:], in_=one[:], func=ACT.Abs_reciprocal_sqrt, bias=1.0)
+
+        def bank(i, name):
+            return psum.tile([P, PACK * TC], F32, name=name, tag="bank%d" % i)
+
+        def by_token(t):
+            return t[:].rearrange("p (j b k) -> p b j k", j=PACK, k=4)
+
+        def interleaved(t):
+            return t[:].rearrange("p (b k j) -> p b j k", j=PACK, k=4)
+
+        st = {}
+
+        def mm_b(c):
+            b = bank(c, "b%d" % c)
+            for j in range(PACK):
+                nc.tensor.matmul_mx(
+                    out=cols(b, j * TC), lhsT=fp8(st["wc"], j * P), lhsT_scale=cols(st["wc_s"], j * P),
+                    rhs=fp4(xq, c * TC), rhs_scale=cols(xq_s, c * TC), start=True, stop=True,
+                )
+            st["b", c] = b
+
+        def mm_a(c):
+            a = bank(4 + c, "a%d" % c)
+            for j in range(PACK):
+                for g in range(2):
+                    nc.tensor.matmul_mx(
+                        out=cols(a, j * TC), lhsT=fp8(st["wa", g], j * P), lhsT_scale=cols(st["wa_s"], g * W + j * P),
+                        rhs=fp4(xt, g * W + c * TC), rhs_scale=cols(xt_s, g * W + c * TC), start=(g == 0), stop=(g == 1),
+                    )
+            st["a", c] = a
+
+        def root(c):
+            d = sb("d%d" % c, [P, W], F32)
+            nc.scalar.activation(out=d[:], in_=st["b", c][:], func=ACT.Abs)
+            s = sb("s%d" % c, [P, W], F32)
+            nc.scalar.activation(out=s[:], in_=d[:], func=ACT.Abs_reciprocal_sqrt, bias=1.0)
+            st["s", c] = s
+
+        def factor(c):
+            f = sb("f%d" % c, [P, W], F32)
+            s = st["s", c]
+            for j in range(PACK):
+                nc.vector.scalar_tensor_tensor(
+                    out=cols(f, j * TC), in0=cols(s, j * TC), scalar=us_t[:, j : j + 1], in1=cols(s, j * TC),
+                    op0=ALU.mult, op1=ALU.mult,
+                )
+            st["f", c] = f
+
+        def hidden(c):
+            h = sb("h%d" % c, [P, W], BF16)
+            nc.vector.tensor_tensor(out=interleaved(h), in0=by_token(st["a", c]), in1=by_token(st["f", c]), op=ALU.mult)
+            st["h", c] = h
+
+        def quant_hidden(c):
+            hq = sb("hq%d" % c, [P, TC], I32)
+            hs = sb("hs%d" % c, [P, TC], U8)
+            nc.vector.quantize_mx(out=hq[:].bitcast(FP8X4), scales=hs[:], in_=st["h", c][:])
+            st["hq", c] = (hq, hs)
+
+        def mm_skip(c):
+            y = bank(c, "y%d" % c)
+            for i in range(PACK):
+                for g in range(2):
+                    nc.tensor.matmul_mx(
+                        out=cols(y, i * TC), lhsT=fp8(st["wy", g], i * P), lhsT_scale=cols(st["wy_s"], g * W + i * P),
+                        rhs=fp4(xt, g * W + c * TC), rhs_scale=cols(xt_s, g * W + c * TC),
+                        start=(i == 0 and g == 0), stop=False,
+                    )
+            st["y", c] = y
+
+        def mm_hid(c):
+            hq, hs = st["hq", c]
+            for i in range(PACK):
+                nc.tensor.matmul_mx(
+                    out=cols(st["y", c], i * TC), lhsT=fp4(st["wb"], i * P), lhsT_scale=cols(st["wb_s"], i * P),
+                    rhs=hq[:].bitcast(FP8X4), rhs_scale=hs[:], start=False, stop=(i == PACK - 1),
+                )
+
+        out_rows = out_0.rearrange("(p i) t -> p i t", i=PACK)
+        yq = sb("yq", [P, T], I32)
+        ys = sb("ys", [P, T], U8)
+
+        def copy_out(c):
+            yf = sb("yf%d" % c, [P, W], F32)
+            nc.scalar.copy(out=yf[:], in_=st["y", c][:])
+            st["yf", c] = yf
+
+        def store_out(c, queue):
+            queue.dma_start(out=out_rows[:, :, c * TC : (c + 1) * TC], in_=st["yf", c][:].rearrange("p (i t) -> p i t", i=PACK))
+
+        def round_scalar(c):
+            yb = sb("yb%d" % c, [P, W], BF16)
+            nc.scalar.copy(out=interleaved(yb), in_=by_token(st["y", c]))
+            st["yb", c] = yb
+
+        def round_vector(c):
+            yb = sb("yb%d" % c, [P, W], BF16)
+            nc.vector.tensor_copy(out=interleaved(yb), in_=by_token(st["yf", c]))
+            st["yb", c] = yb
+
+        def quant_out(c):
+            nc.vector.quantize_mx(out=cols(yq, c * TC).bitcast(FP8X4), scales=cols(ys, c * TC), in_=st["yb", c][:])
+
+        codes_out = out_1.rearrange("g p c t -> p (g c t)").bitcast(I32)
+
+        def store_codes(c0, c1, queue):
+            queue.dma_start(out=codes_out[:, c0 * TC : c1 * TC], in_=yq[:, c0 * TC : c1 * TC])
+
+        def store_scales(q, queue):
+            queue.dma_start(out=out_2[0, 4 * q : 4 * q + 4, :].bitcast(I32), in_=ys[32 * q : 32 * q + 4, :].bitcast(I32))
+
+        st["wc_s"] = deal_scales("wc_s", wc_s_raw, 1)
+        st["wc"] = deal_words("wc", wc_raw, 0)
+        for c in range(CHUNKS):
+            mm_b(c)
+        st["wa", 0] = deal_words("wa0", wa_raw, 0)
+        st["wa", 1] = deal_words("wa1", wa_raw, 1)
+        st["wa_s"] = deal_scales("wa_s", wa_s_raw, 2)
+        for c in range(CHUNKS):
+            root(c)
+        for c in range(CHUNKS):
+            mm_a(c)
+        factor(0)
+        hidden(0)
+        st["wb"] = deal_fp4("wb", wb_raw)
+        quant_hidden(0)
+        st["wy", 0] = deal_words("wy0", wy_raw, 0)
+        st["wy", 1] = deal_words("wy1", wy_raw, 1)
+        factor(1)
+        hidden(1)
+        st["wb_s"] = deal_scales("wb_s", wb_s_raw, 1)
+        quant_hidden(1)
+        st["wy_s"] = deal_scales("wy_s", wy_s_raw, 2)
+        mm_skip(0)
+        mm_hid(0)
+        mm_skip(1)
+        mm_hid(1)
+        mm_skip(2)
+        mm_skip(3)
+        factor(2)
+        hidden(2)
+        round_scalar(0)
+        copy_out(0)
+        store_out(0, nc.sync)
+        factor(3)
+        quant_hidden(2)
+        mm_hid(2)
+        hidden(3)
+        round_scalar(1)
+        copy_out(1)
+        store_out(1, nc.sync)
+        quant_out(0)
+        quant_hidden(3)
+        mm_hid(3)
+        quant_out(1)
+        store_codes(0, 2, nc.sync)
+        copy_out(2)
+        store_out(2, nc.sync)
+        round_vector(2)
+        copy_out(3)
+        store_out(3, nc.sync)
+        quant_out(2)
+        round_vector(3)
+        quant_out(3)
+        store_codes(2, 4, nc.scalar)
+        store_scales(0, nc.sync)
+        store_scales(1, nc.scalar)
+        store_scales(2, nc.sync)
+        store_scales(3, nc.scalar)

@@ -12,12 +12,16 @@ ACT = mybir.ActivationFunctionType
 ALU = mybir.AluOpType
 
 K, L, T, R, N = 1024, 512, 512, 512, 512
+FLOPS = 2 * T * (K * R + L * R + R * N + K * N)
+
 P = 128
 PACK = 4
 W = 512
 TC = 128
 CHUNKS = T // TC
-FLOPS = 2 * T * (K * R + L * R + R * N + K * N)
+K_PASSES = K // (P * PACK)
+QUADRANTS = range(4)
+LINE = 16
 
 
 def tile_mix_hidden_divided_hidden_pl_kernel(
@@ -30,266 +34,266 @@ def tile_mix_hidden_divided_hidden_pl_kernel(
         psum = ctx.enter_context(tc.psum_pool(name="psum", bufs=1))
         ctx.enter_context(tc.manual_schedule())
 
-        def sb(name, shape, dtype):
-            return keep.tile(shape, dtype, name=name, align_bytes=64)
+        def sbuf(name, columns, dtype):
+            return keep.tile([P, columns], dtype, name=name, align_bytes=64)
 
-        def plane(name, passes):
-            t = sb(name, [P, passes * W], U8)
-            nc.vector.memset(t[:].bitcast(I32), 0)
-            return t
+        def bank(index, name):
+            return psum.tile([P, PACK * TC], F32, name=name, tag="bank%d" % index)
 
-        def load_scales(queue, t, scales, quads=range(4)):
-            passes = scales.shape[0]
-            for q in quads:
-                queue.dma_start(
-                    out=t[32 * q : 32 * q + 4, :].bitcast(I32).rearrange("r (g c) -> r g c", g=passes),
+        def cols(view, start):
+            return view[:, start : start + P]
+
+        def fp8(words, start):
+            return cols(words, start).bitcast(FP8X4)
+
+        def fp4(word_bytes, start):
+            return word_bytes[:, 2 * start : 2 * (start + P)].bitcast(FP4X4)
+
+        def as_t_i(tile):
+            return tile[:].rearrange("p (t i) -> p t i", i=PACK)
+
+        def across_groups(tile):
+            return tile[:].rearrange("p (i t) -> p t i", i=PACK)
+
+        b_planes = sbuf("b_planes", 3 * W, U8)
+        a_planes = sbuf("a_planes", 6 * W, U8)
+        y_planes = sbuf("y_planes", 6 * W, U8)
+        wc_s_raw, xq_s, wc_s = b_planes[:, 0:W], b_planes[:, W : 2 * W], b_planes[:, 2 * W : 3 * W]
+        wa_s_raw, xt_s, wa_s = a_planes[:, 0 : 2 * W], a_planes[:, 2 * W : 4 * W], a_planes[:, 4 * W : 6 * W]
+        wb_s_raw, wy_s_raw = y_planes[:, 0:W], y_planes[:, W : 3 * W]
+        wb_s, wy_s = y_planes[:, 3 * W : 4 * W], y_planes[:, 4 * W : 6 * W]
+        nc.vector.memset(b_planes[:, 0 : 2 * W].bitcast(I32), 0)
+        one = sbuf("one", 1, F32)
+        nc.vector.memset(one[:], 1.0)
+        nc.vector.memset(a_planes[:, 0 : 4 * W].bitcast(I32), 0)
+        nc.vector.memset(y_planes[:, 0 : 3 * W].bitcast(I32), 0)
+
+        def load_scales(plane, scales, quadrants):
+            for q in quadrants:
+                nc.sync.dma_start(
+                    out=plane[32 * q : 32 * q + 4, :].bitcast(I32).rearrange("r (g c) -> r g c", g=scales.shape[0]),
                     in_=scales[:, 4 * q : 4 * q + 4, :].bitcast(I32).rearrange("g r c -> r g c"),
                 )
 
         def load_fp8(queue, name, words):
             passes = words.shape[0]
-            t = sb(name, [P, passes * W], I32)
+            tile = sbuf(name, passes * W, I32)
             queue.dma_start(
-                out=t[:].rearrange("p (g c) -> p g c", g=passes),
-                in_=words.rearrange("g p c t -> p g (c t)").bitcast(I32),
+                out=tile[:].rearrange("p (g c) -> p g c", g=passes),
+                in_=words.rearrange("g p c i -> p g (c i)").bitcast(I32),
             )
-            return t
+            return tile
 
         def load_fp4(queue, name, words):
             passes = words.shape[0]
-            t = sb(name, [P, passes * 2 * W], U8)
+            tile = sbuf(name, passes * 2 * W, U8)
             queue.dma_start(
-                out=t[:].bitcast(I32).rearrange("p (g c) -> p g c", g=passes),
+                out=tile[:].bitcast(I32).rearrange("p (g c) -> p g c", g=passes),
                 in_=words.bitcast(I32).rearrange("g p c -> p g c"),
             )
-            return t
+            return tile
 
-        def deal_words(name, raw, g):
-            t = sb(name, [P, W], I32)
-            nc.vector.tensor_copy(
-                out=t[:].rearrange("p (j b k) -> p b j k", j=PACK, k=4),
-                in_=raw[:, g * W : (g + 1) * W].rearrange("p (b k j) -> p b j k", j=PACK, k=4),
-            )
-            return t
+        us_t = sbuf("us_t", PACK, F32)
+        nc.gpsimd.dma_start(out=us_t[:], in_=us.rearrange("(p i) o -> p (i o)", i=PACK))
 
-        def deal_scales(name, raw, passes):
-            t = sb(name, [P, passes * W], U8)
-            nc.vector.tensor_copy(
-                out=t[:].rearrange("p (g j b k) -> p g b j k", g=passes, j=PACK, k=16),
-                in_=raw[:].rearrange("p (g b k j) -> p g b j k", g=passes, j=PACK, k=16),
-            )
-            return t
-
-        def deal_fp4(name, raw):
-            t = sb(name, [P, 2 * W], U8)
-            nc.vector.tensor_copy(
-                out=t[:].rearrange("p (j b k e) -> p b j k e", j=PACK, k=8, e=2),
-                in_=raw[:].rearrange("p (b k j e) -> p b j k e", j=PACK, k=8, e=2),
-            )
-            return t
-
-        def fp8(t, c0):
-            return t[:, c0 : c0 + P].bitcast(FP8X4)
-
-        def fp4(t, c0):
-            return t[:, 2 * c0 : 2 * (c0 + P)].bitcast(FP4X4)
-
-        def cols(t, c0):
-            return t[:, c0 : c0 + P]
-
-        wc_s_raw = plane("wc_s_raw", 1)
-        xq_s = plane("xq_s", 1)
-        wa_s_raw = plane("wa_s_raw", 2)
-        xt_s = plane("xt_s", 2)
-        wb_s_raw = plane("wb_s_raw", 1)
-        wy_s_raw = plane("wy_s_raw", 2)
-
-        one = sb("one", [P, 1], F32)
-        nc.gpsimd.memset(one[:], 1.0)
-        us_t = sb("us_t", [P, PACK], F32)
-        nc.gpsimd.dma_start(out=us_t[:], in_=us.rearrange("(p j) o -> p (j o)", j=PACK))
-
-        wc_raw = load_fp8(nc.scalar, "wc_raw", wc_words)
+        load_scales(wc_s_raw, wc_scales, QUADRANTS)
+        load_scales(xq_s, xq_scales, QUADRANTS[:1])
         xq = load_fp4(nc.scalar, "xq", xq_words)
-        load_scales(nc.sync, wc_s_raw, wc_scales)
-        load_scales(nc.sync, xq_s, xq_scales)
+        wc_raw = load_fp8(nc.scalar, "wc_raw", wc_words)
+        warm = sbuf("warm", 1, F32)
+        nc.scalar.activation(out=warm[:], in_=one[:], func=ACT.Abs_reciprocal_sqrt, bias=1.0)
         wa_raw = load_fp8(nc.sync, "wa_raw", wa_words)
-        load_scales(nc.sync, wa_s_raw, wa_scales)
+
+        load_scales(xq_s, xq_scales, QUADRANTS[1:])
+        load_scales(wa_s_raw, wa_scales, QUADRANTS[:2])
         xt = load_fp4(nc.sync, "xt", xt_words)
-        load_scales(nc.sync, xt_s, xt_scales)
+        load_scales(wa_s_raw, wa_scales, QUADRANTS[2:])
+
+        load_scales(xt_s, xt_scales, QUADRANTS)
         wb_raw = load_fp4(nc.sync, "wb_raw", wb_words)
         wy_raw = load_fp8(nc.sync, "wy_raw", wy_words)
-        load_scales(nc.sync, wb_s_raw, wb_scales)
-        load_scales(nc.sync, wy_s_raw, wy_scales)
+        load_scales(wy_s_raw, wy_scales, QUADRANTS)
+        load_scales(wb_s_raw, wb_scales, QUADRANTS)
 
-        warm = sb("warm", [P, 1], F32)
-        nc.scalar.activation(out=warm[:], in_=one[:], func=ACT.Abs_reciprocal_sqrt, bias=1.0)
+        def deal_fp8(name, raw):
+            run = LINE // 4
+            dealt = []
+            for g in range(raw.shape[1] // W):
+                tile = sbuf("%s%d" % (name, g), W, I32)
+                nc.vector.tensor_copy(
+                    out=tile[:].rearrange("p (i b k) -> p b i k", i=PACK, k=run),
+                    in_=raw[:, g * W : (g + 1) * W].rearrange("p (b k i) -> p b i k", i=PACK, k=run),
+                )
+                dealt.append(tile)
+            return dealt
 
-        def bank(i, name):
-            return psum.tile([P, PACK * TC], F32, name=name, tag="bank%d" % i)
+        def deal_fp4(name, raw):
+            run = LINE // 2
+            tile = sbuf(name, 2 * W, U8)
+            nc.vector.tensor_copy(
+                out=tile[:].rearrange("p (i b k e) -> p b i k e", i=PACK, k=run, e=2),
+                in_=raw[:].rearrange("p (b k i e) -> p b i k e", i=PACK, k=run, e=2),
+            )
+            return tile
 
-        def by_token(t):
-            return t[:].rearrange("p (j b k) -> p b j k", j=PACK, k=4)
+        def deal_scales(dealt, raw):
+            passes = raw.shape[1] // W
+            nc.vector.tensor_copy(
+                out=dealt.rearrange("p (g i b k) -> p g b i k", g=passes, i=PACK, k=LINE),
+                in_=raw.rearrange("p (g b k i) -> p g b i k", g=passes, i=PACK, k=LINE),
+            )
 
-        def interleaved(t):
-            return t[:].rearrange("p (b k j) -> p b j k", j=PACK, k=4)
+        deal_scales(wc_s, wc_s_raw)
+        wc = deal_fp8("wc", wc_raw)
+        wa = deal_fp8("wa", wa_raw)
+        deal_scales(wa_s, wa_s_raw)
+        wb = deal_fp4("wb", wb_raw)
 
-        st = {}
-
-        def mm_b(c):
-            b = bank(c, "b%d" % c)
-            for j in range(PACK):
+        b_bank, magnitude, root, recip = {}, {}, {}, {}
+        for c in range(CHUNKS):
+            b_bank[c] = bank(c, "b%d" % c)
+            for i in range(PACK):
                 nc.tensor.matmul_mx(
-                    out=cols(b, j * TC), lhsT=fp8(st["wc"], j * P), lhsT_scale=cols(st["wc_s"], j * P),
+                    out=cols(b_bank[c], i * TC), lhsT=fp8(wc[0], i * P), lhsT_scale=cols(wc_s, i * P),
                     rhs=fp4(xq, c * TC), rhs_scale=cols(xq_s, c * TC), start=True, stop=True,
                 )
-            st["b", c] = b
 
-        def mm_a(c):
-            a = bank(4 + c, "a%d" % c)
-            for j in range(PACK):
-                for g in range(2):
-                    nc.tensor.matmul_mx(
-                        out=cols(a, j * TC), lhsT=fp8(st["wa", g], j * P), lhsT_scale=cols(st["wa_s"], g * W + j * P),
-                        rhs=fp4(xt, g * W + c * TC), rhs_scale=cols(xt_s, g * W + c * TC), start=(g == 0), stop=(g == 1),
-                    )
-            st["a", c] = a
+        def take_magnitude(c):
+            magnitude[c] = sbuf("magnitude%d" % c, W, F32)
+            nc.scalar.activation(out=as_t_i(magnitude[c]), in_=across_groups(b_bank[c]), func=ACT.Abs)
 
-        def root(c):
-            d = sb("d%d" % c, [P, W], F32)
-            nc.scalar.activation(out=d[:], in_=st["b", c][:], func=ACT.Abs)
-            s = sb("s%d" % c, [P, W], F32)
-            nc.scalar.activation(out=s[:], in_=d[:], func=ACT.Abs_reciprocal_sqrt, bias=1.0)
-            st["s", c] = s
+        def take_root(c):
+            root[c] = sbuf("root%d" % c, W, F32)
+            nc.scalar.activation(out=root[c][:], in_=magnitude[c][:], func=ACT.Abs_reciprocal_sqrt, bias=1.0)
 
-        def factor(c):
-            f = sb("f%d" % c, [P, W], F32)
-            s = st["s", c]
-            for j in range(PACK):
-                nc.vector.scalar_tensor_tensor(
-                    out=cols(f, j * TC), in0=cols(s, j * TC), scalar=us_t[:, j : j + 1], in1=cols(s, j * TC),
-                    op0=ALU.mult, op1=ALU.mult,
-                )
-            st["f", c] = f
+        def take_square(c):
+            recip[c] = sbuf("recip%d" % c, W, F32)
+            nc.scalar.activation(out=recip[c][:], in_=root[c][:], func=ACT.Square)
 
-        def hidden(c):
-            h = sb("h%d" % c, [P, W], BF16)
-            nc.vector.tensor_tensor(out=interleaved(h), in0=by_token(st["a", c]), in1=by_token(st["f", c]), op=ALU.mult)
-            st["h", c] = h
+        for step in range(CHUNKS + 2):
+            if step < CHUNKS:
+                take_magnitude(step)
+            if 1 <= step <= CHUNKS:
+                take_root(step - 1)
+            if step >= 2:
+                take_square(step - 2)
 
-        def quant_hidden(c):
-            hq = sb("hq%d" % c, [P, TC], I32)
-            hs = sb("hs%d" % c, [P, TC], U8)
-            nc.vector.quantize_mx(out=hq[:].bitcast(FP8X4), scales=hs[:], in_=st["h", c][:])
-            st["hq", c] = (hq, hs)
-
-        def mm_skip(c):
-            y = bank(c, "y%d" % c)
+        a_bank = {}
+        for c in range(CHUNKS):
+            a_bank[c] = bank(CHUNKS + c, "a%d" % c)
             for i in range(PACK):
-                for g in range(2):
+                for g in range(K_PASSES):
                     nc.tensor.matmul_mx(
-                        out=cols(y, i * TC), lhsT=fp8(st["wy", g], i * P), lhsT_scale=cols(st["wy_s"], g * W + i * P),
+                        out=cols(a_bank[c], i * TC), lhsT=fp8(wa[g], i * P), lhsT_scale=cols(wa_s, g * W + i * P),
+                        rhs=fp4(xt, g * W + c * TC), rhs_scale=cols(xt_s, g * W + c * TC),
+                        start=(g == 0), stop=(g == K_PASSES - 1),
+                    )
+
+        a_us, hid, hid_codes, hid_s = {}, {}, {}, {}
+
+        def scale_a(c):
+            a_us[c] = sbuf("a_us%d" % c, W, F32)
+            nc.vector.tensor_tensor(
+                out=as_t_i(a_us[c]), in0=across_groups(a_bank[c]),
+                in1=us_t[:].unsqueeze(1).to_broadcast([P, TC, PACK]), op=ALU.mult,
+            )
+
+        def make_hid(c):
+            hid[c] = sbuf("hid%d" % c, W, BF16)
+            nc.vector.tensor_tensor(out=hid[c][:], in0=a_us[c][:], in1=recip[c][:], op=ALU.mult)
+
+        def quantise_hid(c):
+            hid_codes[c] = sbuf("hid_codes%d" % c, TC, I32)
+            hid_s[c] = sbuf("hid_s%d" % c, TC, U8)
+            nc.vector.quantize_mx(out=hid_codes[c][:].bitcast(FP8X4), scales=hid_s[c][:], in_=hid[c][:])
+
+        y_bank, y_f32, y_bf16 = {}, {}, {}
+
+        def skip_product(c):
+            y_bank[c] = bank(c, "y%d" % c)
+            for i in range(PACK):
+                for g in range(K_PASSES):
+                    nc.tensor.matmul_mx(
+                        out=cols(y_bank[c], i * TC), lhsT=fp8(wy[g], i * P), lhsT_scale=cols(wy_s, g * W + i * P),
                         rhs=fp4(xt, g * W + c * TC), rhs_scale=cols(xt_s, g * W + c * TC),
                         start=(i == 0 and g == 0), stop=False,
                     )
-            st["y", c] = y
 
-        def mm_hid(c):
-            hq, hs = st["hq", c]
+        def hid_product(c):
             for i in range(PACK):
                 nc.tensor.matmul_mx(
-                    out=cols(st["y", c], i * TC), lhsT=fp4(st["wb"], i * P), lhsT_scale=cols(st["wb_s"], i * P),
-                    rhs=hq[:].bitcast(FP8X4), rhs_scale=hs[:], start=False, stop=(i == PACK - 1),
+                    out=cols(y_bank[c], i * TC), lhsT=fp4(wb, i * P), lhsT_scale=cols(wb_s, i * P),
+                    rhs=hid_codes[c][:].bitcast(FP8X4), rhs_scale=hid_s[c][:], start=False, stop=(i == PACK - 1),
                 )
 
         out_rows = out_0.rearrange("(p i) t -> p i t", i=PACK)
-        yq = sb("yq", [P, T], I32)
-        ys = sb("ys", [P, T], U8)
+        out_words = out_1.rearrange("g p c i -> p (g c i)").bitcast(I32)
+        y_codes = sbuf("y_codes", T, I32)
+        y_s = sbuf("y_s", T, U8)
 
-        def copy_out(c):
-            yf = sb("yf%d" % c, [P, W], F32)
-            nc.scalar.copy(out=yf[:], in_=st["y", c][:])
-            st["yf", c] = yf
+        def store_out(c):
+            y_f32[c] = sbuf("y_f32_%d" % c, W, F32)
+            nc.scalar.copy(out=y_f32[c][:], in_=y_bank[c][:])
+            nc.sync.dma_start(
+                out=out_rows[:, :, c * TC : (c + 1) * TC], in_=y_f32[c][:].rearrange("p (i t) -> p i t", i=PACK)
+            )
 
-        def store_out(c, queue):
-            queue.dma_start(out=out_rows[:, :, c * TC : (c + 1) * TC], in_=st["yf", c][:].rearrange("p (i t) -> p i t", i=PACK))
+        def round_on_scalar(c):
+            y_bf16[c] = sbuf("y_bf16_%d" % c, W, BF16)
+            nc.scalar.copy(out=as_t_i(y_bf16[c]), in_=across_groups(y_bank[c]))
 
-        def round_scalar(c):
-            yb = sb("yb%d" % c, [P, W], BF16)
-            nc.scalar.copy(out=interleaved(yb), in_=by_token(st["y", c]))
-            st["yb", c] = yb
+        def round_on_vector(c):
+            run = LINE // 4
+            y_bf16[c] = sbuf("y_bf16_%d" % c, W, BF16)
+            nc.vector.tensor_copy(
+                out=y_bf16[c][:].rearrange("p (b k i) -> p b i k", i=PACK, k=run),
+                in_=y_f32[c][:].rearrange("p (i b k) -> p b i k", i=PACK, k=run),
+            )
 
-        def round_vector(c):
-            yb = sb("yb%d" % c, [P, W], BF16)
-            nc.vector.tensor_copy(out=interleaved(yb), in_=by_token(st["yf", c]))
-            st["yb", c] = yb
+        def quantise_out(c):
+            nc.vector.quantize_mx(out=fp8(y_codes, c * TC), scales=cols(y_s, c * TC), in_=y_bf16[c][:])
 
-        def quant_out(c):
-            nc.vector.quantize_mx(out=cols(yq, c * TC).bitcast(FP8X4), scales=cols(ys, c * TC), in_=st["yb", c][:])
+        def store_codes(queue, first, last):
+            span = slice(first * TC, (last + 1) * TC)
+            queue.dma_start(out=out_words[:, span], in_=y_codes[:, span])
 
-        codes_out = out_1.rearrange("g p c t -> p (g c t)").bitcast(I32)
-
-        def store_codes(c0, c1, queue):
-            queue.dma_start(out=codes_out[:, c0 * TC : c1 * TC], in_=yq[:, c0 * TC : c1 * TC])
-
-        def store_scales(q, queue):
-            queue.dma_start(out=out_2[0, 4 * q : 4 * q + 4, :].bitcast(I32), in_=ys[32 * q : 32 * q + 4, :].bitcast(I32))
-
-        st["wc_s"] = deal_scales("wc_s", wc_s_raw, 1)
-        st["wc"] = deal_words("wc", wc_raw, 0)
-        for c in range(CHUNKS):
-            mm_b(c)
-        st["wa", 0] = deal_words("wa0", wa_raw, 0)
-        st["wa", 1] = deal_words("wa1", wa_raw, 1)
-        st["wa_s"] = deal_scales("wa_s", wa_s_raw, 2)
-        for c in range(CHUNKS):
-            root(c)
-        for c in range(CHUNKS):
-            mm_a(c)
-        factor(0)
-        hidden(0)
-        st["wb"] = deal_fp4("wb", wb_raw)
-        quant_hidden(0)
-        st["wy", 0] = deal_words("wy0", wy_raw, 0)
-        st["wy", 1] = deal_words("wy1", wy_raw, 1)
-        factor(1)
-        hidden(1)
-        st["wb_s"] = deal_scales("wb_s", wb_s_raw, 1)
-        quant_hidden(1)
-        st["wy_s"] = deal_scales("wy_s", wy_s_raw, 2)
-        mm_skip(0)
-        mm_hid(0)
-        mm_skip(1)
-        mm_hid(1)
-        mm_skip(2)
-        mm_skip(3)
-        factor(2)
-        hidden(2)
-        round_scalar(0)
-        copy_out(0)
-        store_out(0, nc.sync)
-        factor(3)
-        quant_hidden(2)
-        mm_hid(2)
-        hidden(3)
-        round_scalar(1)
-        copy_out(1)
-        store_out(1, nc.sync)
-        quant_out(0)
-        quant_hidden(3)
-        mm_hid(3)
-        quant_out(1)
-        store_codes(0, 2, nc.sync)
-        copy_out(2)
-        store_out(2, nc.sync)
-        round_vector(2)
-        copy_out(3)
-        store_out(3, nc.sync)
-        quant_out(2)
-        round_vector(3)
-        quant_out(3)
-        store_codes(2, 4, nc.scalar)
-        store_scales(0, nc.sync)
-        store_scales(1, nc.scalar)
-        store_scales(2, nc.sync)
-        store_scales(3, nc.scalar)
+        scale_a(0)
+        wy = deal_fp8("wy", wy_raw)
+        deal_scales(wy_s, wy_s_raw)
+        make_hid(0)
+        scale_a(1)
+        quantise_hid(0)
+        deal_scales(wb_s, wb_s_raw)
+        scale_a(2)
+        skip_product(0)
+        hid_product(0)
+        skip_product(1)
+        skip_product(2)
+        make_hid(1)
+        scale_a(3)
+        quantise_hid(1)
+        hid_product(1)
+        round_on_scalar(0)
+        store_out(0)
+        skip_product(3)
+        make_hid(2)
+        make_hid(3)
+        quantise_hid(2)
+        hid_product(2)
+        quantise_out(0)
+        quantise_hid(3)
+        hid_product(3)
+        round_on_scalar(1)
+        store_out(1)
+        store_out(2)
+        quantise_out(1)
+        store_codes(nc.sync, 0, 1)
+        round_on_vector(2)
+        store_out(3)
+        round_on_vector(3)
+        quantise_out(2)
+        quantise_out(3)
+        store_codes(nc.sync, 2, 3)
+        for q in QUADRANTS:
+            queue = nc.scalar if q % 2 else nc.sync
+            queue.dma_start(out=out_2[0, 4 * q : 4 * q + 4, :].bitcast(I32), in_=y_s[32 * q : 32 * q + 4, :].bitcast(I32))

from contextlib import ExitStack

import concourse.mybir as mybir

F32 = mybir.dt.float32
BF16 = mybir.dt.bfloat16
I32 = mybir.dt.int32
U8 = mybir.dt.uint8
FP8X4 = mybir.dt.float8_e4m3fn_x4
FP4X4 = mybir.dt.float4_e2m1fn_x4
ACT = mybir.ActivationFunctionType
ALU = mybir.AluOpType

K, L, T, R, N = 1024, 512, 512, 512, 512
FLOPS = 2 * T * (K * R + L * R + R * N + K * N)

P = 128
PACK = 4
W = 512
TC = 128
CHUNKS = T // TC
K_PASSES = K // (P * PACK)
QUADRANTS = range(4)
LINE = 16


def tile_mix_hidden_divided_hidden_pl_kernel(
    tc, xt_words, xt_scales, wa_words, wa_scales, xq_words, xq_scales, wc_words, wc_scales,
    us, wb_words, wb_scales, wy_words, wy_scales, out_0, out_1, out_2,
):
    nc = tc.nc
    with ExitStack() as ctx:
        keep = ctx.enter_context(tc.tile_pool(name="keep", bufs=1))
        psum = ctx.enter_context(tc.psum_pool(name="psum", bufs=1))
        ctx.enter_context(tc.manual_schedule())

        def sbuf(name, columns, dtype):
            return keep.tile([P, columns], dtype, name=name, align_bytes=64)

        def bank(index, name):
            return psum.tile([P, PACK * TC], F32, name=name, tag="bank%d" % index)

        def cols(view, start):
            return view[:, start : start + P]

        def fp8(words, start):
            return cols(words, start).bitcast(FP8X4)

        def fp4(word_bytes, start):
            return word_bytes[:, 2 * start : 2 * (start + P)].bitcast(FP4X4)

        def as_t_i(tile):
            return tile[:].rearrange("p (t i) -> p t i", i=PACK)

        def across_groups(tile):
            return tile[:].rearrange("p (i t) -> p t i", i=PACK)

        b_planes = sbuf("b_planes", 3 * W, U8)
        a_planes = sbuf("a_planes", 6 * W, U8)
        y_planes = sbuf("y_planes", 6 * W, U8)
        wc_s_raw, xq_s, wc_s = b_planes[:, 0:W], b_planes[:, W : 2 * W], b_planes[:, 2 * W : 3 * W]
        wa_s_raw, xt_s, wa_s = a_planes[:, 0 : 2 * W], a_planes[:, 2 * W : 4 * W], a_planes[:, 4 * W : 6 * W]
        wb_s_raw, wy_s_raw = y_planes[:, 0:W], y_planes[:, W : 3 * W]
        wb_s, wy_s = y_planes[:, 3 * W : 4 * W], y_planes[:, 4 * W : 6 * W]
        nc.vector.memset(b_planes[:, 0 : 2 * W].bitcast(I32), 0)
        one = sbuf("one", 1, F32)
        nc.vector.memset(one[:], 1.0)
        nc.vector.memset(a_planes[:, 0 : 4 * W].bitcast(I32), 0)
        nc.vector.memset(y_planes[:, 0 : 3 * W].bitcast(I32), 0)

        def load_scales(plane, scales, quadrants):
            for q in quadrants:
                nc.sync.dma_start(
                    out=plane[32 * q : 32 * q + 4, :].bitcast(I32).rearrange("r (g c) -> r g c", g=scales.shape[0]),
                    in_=scales[:, 4 * q : 4 * q + 4, :].bitcast(I32).rearrange("g r c -> r g c"),
                )

        def load_fp8(queue, name, words):
            passes = words.shape[0]
            tile = sbuf(name, passes * W, I32)
            queue.dma_start(
                out=tile[:].rearrange("p (g c) -> p g c", g=passes),
                in_=words.rearrange("g p c i -> p g (c i)").bitcast(I32),
            )
            return tile

        def load_fp4(queue, name, words):
            passes = words.shape[0]
            tile = sbuf(name, passes * 2 * W, U8)
            queue.dma_start(
                out=tile[:].bitcast(I32).rearrange("p (g c) -> p g c", g=passes),
                in_=words.bitcast(I32).rearrange("g p c -> p g c"),
            )
            return tile

        us_t = sbuf("us_t", PACK, F32)
        nc.gpsimd.dma_start(out=us_t[:], in_=us.rearrange("(p i) o -> p (i o)", i=PACK))

        load_scales(wc_s_raw, wc_scales, QUADRANTS)
        load_scales(xq_s, xq_scales, QUADRANTS[:1])
        xq = load_fp4(nc.scalar, "xq", xq_words)
        wc_raw = load_fp8(nc.scalar, "wc_raw", wc_words)
        warm = sbuf("warm", 1, F32)
        nc.scalar.activation(out=warm[:], in_=one[:], func=ACT.Abs_reciprocal_sqrt, bias=1.0)
        wa_raw = load_fp8(nc.sync, "wa_raw", wa_words)

        load_scales(xq_s, xq_scales, QUADRANTS[1:])
        load_scales(wa_s_raw, wa_scales, QUADRANTS[:2])
        xt = load_fp4(nc.sync, "xt", xt_words)
        load_scales(wa_s_raw, wa_scales, QUADRANTS[2:])

        load_scales(xt_s, xt_scales, QUADRANTS)
        wb_raw = load_fp4(nc.sync, "wb_raw", wb_words)
        wy_raw = load_fp8(nc.sync, "wy_raw", wy_words)
        load_scales(wy_s_raw, wy_scales, QUADRANTS)
        load_scales(wb_s_raw, wb_scales, QUADRANTS)

        def deal_fp8(name, raw):
            run = LINE // 4
            dealt = []
            for g in range(raw.shape[1] // W):
                tile = sbuf("%s%d" % (name, g), W, I32)
                nc.vector.tensor_copy(
                    out=tile[:].rearrange("p (i b k) -> p b i k", i=PACK, k=run),
                    in_=raw[:, g * W : (g + 1) * W].rearrange("p (b k i) -> p b i k", i=PACK, k=run),
                )
                dealt.append(tile)
            return dealt

        def deal_fp4(name, raw):
            run = LINE // 2
            tile = sbuf(name, 2 * W, U8)
            nc.vector.tensor_copy(
                out=tile[:].rearrange("p (i b k e) -> p b i k e", i=PACK, k=run, e=2),
                in_=raw[:].rearrange("p (b k i e) -> p b i k e", i=PACK, k=run, e=2),
            )
            return tile

        def deal_scales(dealt, raw):
            passes = raw.shape[1] // W
            nc.vector.tensor_copy(
                out=dealt.rearrange("p (g i b k) -> p g b i k", g=passes, i=PACK, k=LINE),
                in_=raw.rearrange("p (g b k i) -> p g b i k", g=passes, i=PACK, k=LINE),
            )

        deal_scales(wc_s, wc_s_raw)
        wc = deal_fp8("wc", wc_raw)
        wa = deal_fp8("wa", wa_raw)
        deal_scales(wa_s, wa_s_raw)
        wb = deal_fp4("wb", wb_raw)

        b_bank, magnitude, root, recip = {}, {}, {}, {}
        for c in range(CHUNKS):
            b_bank[c] = bank(c, "b%d" % c)
            for i in range(PACK):
                nc.tensor.matmul_mx(
                    out=cols(b_bank[c], i * TC), lhsT=fp8(wc[0], i * P), lhsT_scale=cols(wc_s, i * P),
                    rhs=fp4(xq, c * TC), rhs_scale=cols(xq_s, c * TC), start=True, stop=True,
                )

        def take_magnitude(c):
            magnitude[c] = sbuf("magnitude%d" % c, W, F32)
            nc.scalar.activation(out=as_t_i(magnitude[c]), in_=across_groups(b_bank[c]), func=ACT.Abs)

        def take_root(c):
            root[c] = sbuf("root%d" % c, W, F32)
            nc.scalar.activation(out=root[c][:], in_=magnitude[c][:], func=ACT.Abs_reciprocal_sqrt, bias=1.0)

        def take_square(c):
            recip[c] = sbuf("recip%d" % c, W, F32)
            nc.scalar.activation(out=recip[c][:], in_=root[c][:], func=ACT.Square)

        for step in range(CHUNKS + 2):
            if step < CHUNKS:
                take_magnitude(step)
            if 1 <= step <= CHUNKS:
                take_root(step - 1)
            if step >= 2:
                take_square(step - 2)

        a_bank = {}
        for c in range(CHUNKS):
            a_bank[c] = bank(CHUNKS + c, "a%d" % c)
            for i in range(PACK):
                for g in range(K_PASSES):
                    nc.tensor.matmul_mx(
                        out=cols(a_bank[c], i * TC), lhsT=fp8(wa[g], i * P), lhsT_scale=cols(wa_s, g * W + i * P),
                        rhs=fp4(xt, g * W + c * TC), rhs_scale=cols(xt_s, g * W + c * TC),
                        start=(g == 0), stop=(g == K_PASSES - 1),
                    )

        a_us, hid, hid_codes, hid_s = {}, {}, {}, {}

        def scale_a(c):
            a_us[c] = sbuf("a_us%d" % c, W, F32)
            nc.vector.tensor_tensor(
                out=as_t_i(a_us[c]), in0=across_groups(a_bank[c]),
                in1=us_t[:].unsqueeze(1).to_broadcast([P, TC, PACK]), op=ALU.mult,
            )

        def make_hid(c):
            hid[c] = sbuf("hid%d" % c, W, BF16)
            nc.vector.tensor_tensor(out=hid[c][:], in0=a_us[c][:], in1=recip[c][:], op=ALU.mult)

        def quantise_hid(c):
            hid_codes[c] = sbuf("hid_codes%d" % c, TC, I32)
            hid_s[c] = sbuf("hid_s%d" % c, TC, U8)
            nc.vector.quantize_mx(out=hid_codes[c][:].bitcast(FP8X4), scales=hid_s[c][:], in_=hid[c][:])

        y_bank, y_f32, y_bf16 = {}, {}, {}

        def skip_product(c):
            y_bank[c] = bank(c, "y%d" % c)
            for i in range(PACK):
                for g in range(K_PASSES):
                    nc.tensor.matmul_mx(
                        out=cols(y_bank[c], i * TC), lhsT=fp8(wy[g], i * P), lhsT_scale=cols(wy_s, g * W + i * P),
                        rhs=fp4(xt, g * W + c * TC), rhs_scale=cols(xt_s, g * W + c * TC),
                        start=(i == 0 and g == 0), stop=False,
                    )

        def hid_product(c):
            for i in range(PACK):
                nc.tensor.matmul_mx(
                    out=cols(y_bank[c], i * TC), lhsT=fp4(wb, i * P), lhsT_scale=cols(wb_s, i * P),
                    rhs=hid_codes[c][:].bitcast(FP8X4), rhs_scale=hid_s[c][:], start=False, stop=(i == PACK - 1),
                )

        out_rows = out_0.rearrange("(p i) t -> p i t", i=PACK)
        out_words = out_1.rearrange("g p c i -> p (g c i)").bitcast(I32)
        y_codes = sbuf("y_codes", T, I32)
        y_s = sbuf("y_s", T, U8)

        def store_out(c):
            y_f32[c] = sbuf("y_f32_%d" % c, W, F32)
            nc.scalar.copy(out=y_f32[c][:], in_=y_bank[c][:])
            nc.sync.dma_start(
                out=out_rows[:, :, c * TC : (c + 1) * TC], in_=y_f32[c][:].rearrange("p (i t) -> p i t", i=PACK)
            )

        def round_on_scalar(c):
            y_bf16[c] = sbuf("y_bf16_%d" % c, W, BF16)
            nc.scalar.copy(out=as_t_i(y_bf16[c]), in_=across_groups(y_bank[c]))

        def round_on_vector(c):
            run = LINE // 4
            y_bf16[c] = sbuf("y_bf16_%d" % c, W, BF16)
            nc.vector.tensor_copy(
                out=y_bf16[c][:].rearrange("p (b k i) -> p b i k", i=PACK, k=run),
                in_=y_f32[c][:].rearrange("p (i b k) -> p b i k", i=PACK, k=run),
            )

        def quantise_out(c):
            nc.vector.quantize_mx(out=fp8(y_codes, c * TC), scales=cols(y_s, c * TC), in_=y_bf16[c][:])

        def store_codes(queue, first, last):
            span = slice(first * TC, (last + 1) * TC)
            queue.dma_start(out=out_words[:, span], in_=y_codes[:, span])

        scale_a(0)
        wy = deal_fp8("wy", wy_raw)
        deal_scales(wy_s, wy_s_raw)
        make_hid(0)
        scale_a(1)
        quantise_hid(0)
        deal_scales(wb_s, wb_s_raw)
        scale_a(2)
        skip_product(0)
        hid_product(0)
        skip_product(1)
        skip_product(2)
        make_hid(1)
        scale_a(3)
        quantise_hid(1)
        hid_product(1)
        round_on_scalar(0)
        store_out(0)
        skip_product(3)
        make_hid(2)
        make_hid(3)
        quantise_hid(2)
        hid_product(2)
        quantise_out(0)
        quantise_hid(3)
        hid_product(3)
        round_on_scalar(1)
        store_out(1)
        store_out(2)
        quantise_out(1)
        store_codes(nc.sync, 0, 1)
        round_on_vector(2)
        store_out(3)
        round_on_vector(3)
        quantise_out(2)
        quantise_out(3)
        store_codes(nc.sync, 2, 3)
        for q in QUADRANTS:
            queue = nc.scalar if q % 2 else nc.sync
            queue.dma_start(out=out_2[0, 4 * q : 4 * q + 4, :].bitcast(I32), in_=y_s[32 * q : 32 * q + 4, :].bitcast(I32))
